import numpy as np, ml_dtypes
CORES = [1,2,5,7,57,58,61,63,73,74,77,79]
N = 12
W = 64
def setup_inputs(rng):
    return {"x": rng.standard_normal((N, 128, W), dtype=np.float32).astype(ml_dtypes.bfloat16), "a": (7 + rng.standard_normal((N, 128, W), dtype=np.float32) - 9 * (rng.random((N, 128, W)) < 2.0 / (N * W))).astype(ml_dtypes.bfloat16)}
def setup_inputs_big(rng):
    d = setup_inputs(rng)
    for k in ("x",): d[k] = (d[k].astype(np.float32) * 1048576.0).astype(d[k].dtype)
    return d
def setup_inputs_small(rng):
    d = setup_inputs(rng)
    for k in ("x",): d[k] = (d[k].astype(np.float32) * (1 / 1048576.0)).astype(d[k].dtype)
    return d
def setup_inputs_apart(rng):
    d = setup_inputs(rng)
    f = (10.0 ** rng.permutation(np.linspace(-1.5, 1.5, N))).astype(np.float32).reshape(N, 1, 1)
    for k in ("x",): d[k] = (d[k].astype(np.float32) * f).astype(d[k].dtype)
    return d
def reference(x, a):
    X = np.concatenate(list(x.astype(np.float64)), axis=1); G = 1.0 / (1.0 + np.exp(-np.concatenate(list(a.astype(np.float64)), axis=1)))
    h = np.zeros(128); H = np.zeros_like(X)
    for c in range(N * W):
        h = G[:, c] * h + X[:, c]; H[:, c] = h
    return {"y": np.stack([H[:, W * r:W * r + W] for r in range(N)]).astype(ml_dtypes.bfloat16)}

from concourse.bass import DstId, RemoteDMATransfer
from concourse.mybir import AluOpType, AxisListType, ActivationFunctionType

W = 64
NS = 4
NP = 8
RAW_ENGINES = 16
PAIR_ENGINES = 8

SCRATCH = {
    "raw": ("sbuf", [128, NS * 2 * W], "bfloat16"),
    "z": ("sbuf", [128, 2 * (NP + NS * W)], "float32"),
    "loc": ("sbuf", [128, W + 4], "float32"),
    "yy": ("sbuf", [128, NP + NS * W], "bfloat16"),
    "hl": ("sbuf", [128, 8], "bfloat16"),
}
SEMAPHORES = ["lda", "ldx", "sg0", "sx0", "sg1", "sx1", "sloc", "sy", "rawin", "arr", "sent", "st"]


def _bits(mask):
    return [b for b in range(mask.bit_length()) if (mask >> b) & 1]


def _first(mask, n):
    bits = _bits(mask)
    while n > len(bits):
        n //= 2
    m = 0
    for b in bits[:n]:
        m |= 1 << b
    return m


def _pow2(n):
    p = 1
    while 2 * p <= n:
        p *= 2
    return p


def _layout(cores, topo):
    first = topo.chip(cores[0])
    head = [r for r, c in enumerate(cores) if topo.chip(c) == first]
    tail = [r for r in range(len(cores)) if r not in head]
    aggs = [r for r in head if all(topo.may_write(cores[r], cores[t]) for t in tail)]
    serve = {}
    for q in aggs:
        serve[q] = []
    for t in tail:
        near = [q for q in aggs if topo.die(cores[q]) == topo.die(cores[t])] or aggs
        serve[min(near, key=lambda q: len(serve[q]))].append(t)
    return head, tail, aggs, serve


def _sends(j, cores, topo, lay):
    head, tail, aggs, serve = lay

    def common(ds):
        m = topo.mask(cores[j], cores[ds[0]])
        for d in ds[1:]:
            m &= topo.mask(cores[j], cores[d])
        return m

    calls = []
    if j in head:
        raw_to = [q for q in head if q != j and (q in aggs or (q > j and j != head[0]))]
        if raw_to:
            calls.append(("raw", None, [(_first(common(raw_to), RAW_ENGINES), raw_to)]))
        if j == head[0]:
            to = [q for q in head[1:] if q not in aggs]
            if to:
                calls.append(("carry", 0, [(_first(common(to), RAW_ENGINES), to)]))
        if j in aggs and serve[j]:
            m = common(serve[j])
            calls.append(("carry", len(head) - 1, [(_first(m, _pow2(len(_bits(m)))), serve[j])]))
    else:
        later = [t for t in tail if t > j]
        off = [t for t in later if topo.chip(cores[t]) != topo.chip(cores[j])]
        on = [t for t in later if topo.chip(cores[t]) == topo.chip(cores[j])]
        trs = []
        used = 0
        if off:
            m = common(off)
            used = _first(m, _pow2(len(_bits(m))))
            trs.append((used, off))
        if on:
            m = common(on) & ~used
            trs.append((_first(m, min(PAIR_ENGINES, _pow2(len(_bits(m))))), on))
        if trs:
            calls.append(("pair", None, trs))
    return calls


def rank_program(g, core, T, topo):
    r = T.rank_of(core)
    if r is None:
        return
    cores = list(T.cores)
    lay = _layout(cores, topo)
    head, tail, aggs, serve = lay
    S = T.sem
    mult, add = AluOpType.mult, AluOpType.add
    sigmoid = ActivationFunctionType.Sigmoid

    n_in = {"raw": 0, "pair": 0, "carry": 0}
    for j in range(len(cores)):
        if j != r:
            for kind, _, trs in _sends(j, cores, topo, lay):
                for m, ds in trs:
                    if r in ds:
                        n_in[kind] += len(_bits(m))
    n_raw, n_arr = n_in["raw"], n_in["pair"] + n_in["carry"]

    def zx(p0, p1):
        return T.z[:, 2 * p0:2 * p1:2]

    def zg(p0, p1):
        return T.z[:, 2 * p0 + 1:2 * p1:2]

    def ra(s):
        return T.raw[:, 2 * W * s:2 * W * s + W]

    def rx(s):
        return T.raw[:, 2 * W * s + W:2 * W * (s + 1)]

    sent = [0]

    def issue(spec):
        trs = []
        for m, src, dl, sem in spec:
            ids = []
            for d, _ in dl:
                rid, pid, _se = topo.addr(cores[d])
                ids.append(DstId(rid=rid, pnc=pid))
            trs.append(RemoteDMATransfer(dst_ids=ids, dma_engine_mask=m, remote_sem=sem,
                                         srcs=[src], dsts=[ap for _, ap in dl], alu_op=0))
            sent[0] += len(_bits(m))
        g.remote_dma_fused(trs, local_sem=S.sent)

    pos = head.index(r) if r in head else 0
    own = NP + W * pos

    g.sync.dma_start(ra(pos), T.a[:, :]).then_inc(S.lda, 16)
    g.scalar.dma_start(rx(pos), T.x[:, :]).then_inc(S.ldx, 16)
    g.scalar.wait_ge(S.lda, 16)
    g.scalar.activation(zg(own, own + W), ra(pos), sigmoid).then_inc(S.sg0, 1)
    g.vector.wait_ge(S.ldx, 16)
    g.vector.tensor_copy(zx(own, own + W), rx(pos)).then_inc(S.sx0, 1)

    calls = _sends(r, cores, topo, lay)

    if r in head:
        lo = 0 if (r in aggs or pos == 0) else 1
        hi = len(head) if r in aggs else pos + 1
        others = [s for s in range(lo, hi) if s != pos]
        for kind, _, trs in calls:
            if kind == "raw":
                g.wait_ge(S.lda, 16)
                g.wait_ge(S.ldx, 16)
                sl = T.raw[:, 2 * W * pos:2 * W * (pos + 1)]
                issue([(m, sl, [(d, sl) for d in ds], S.rawin) for m, ds in trs])
        if others:
            g.scalar.wait_ge(S.rawin, n_raw)
            g.vector.wait_ge(S.rawin, n_raw)
            for s in others:
                p = NP + W * s
                g.scalar.activation(zg(p, p + W), ra(s), sigmoid).then_inc(S.sg1, 1)
                g.vector.tensor_copy(zx(p, p + W), rx(s)).then_inc(S.sx1, 1)
            g.vector.wait_ge(S.sg1, len(others))
            g.vector.wait_ge(S.sx1, len(others))
        p0, p1 = NP + W * lo, NP + W * hi
    else:
        ti = tail.index(r)
        if calls:
            g.vector.wait_ge(S.sg0, 1)
            g.vector.wait_ge(S.sx0, 1)
            g.vector.tensor_tensor_scan(T.loc[:, 0:W], zg(own, own + W), zx(own, own + W), 0.0, mult, add).then_inc(S.sloc, 1)
            g.vector.tensor_reduce(T.loc[:, W:W + 1], zg(own, own + W), AxisListType.X, mult).then_inc(S.sloc, 1)
            g.wait_ge(S.sloc, 2)
            for kind, _, trs in calls:
                spec = []
                for m, ds in trs:
                    dl = []
                    for d in ds:
                        p = NP - (tail.index(d) - ti)
                        dl.append((d, T.z[:, 2 * p:2 * p + 2]))
                    spec.append((m, T.loc[:, W - 1:W + 1], dl, S.arr))
                issue(spec)
        p0, p1 = NP - ti, NP + W

    g.vector.wait_ge(S.sg0, 1)
    g.vector.wait_ge(S.sx0, 1)
    if n_arr:
        g.vector.wait_ge(S.arr, n_arr)
    init = T.hl[:, 0:1] if n_in["carry"] else 0.0
    g.vector.tensor_tensor_scan(T.yy[:, p0:p1], zg(p0, p1), zx(p0, p1), init, mult, add).then_inc(S.sy, 1)

    g.sync.wait_ge(S.sy, 1)
    g.sync.dma_start(T.y[:, :], T.yy[:, own:own + W]).then_inc(S.st, 16)

    for kind, slot, trs in calls:
        if kind == "carry":
            g.wait_ge(S.sy, 1)
            c = NP + W * (slot + 1) - 1
            issue([(m, T.yy[:, c:c + 1], [(d, T.hl[:, 0:1]) for d in ds], S.arr) for m, ds in trs])
    if sent[0]:
        g.wait_ge(S.sent, sent[0])
    g.sync.wait_ge(S.st, 16)
